import numpy as np
import ml_dtypes


def mxq(x, axis, fmt="e4m3"):
    dtype, down = {"e4m3": (ml_dtypes.float8_e4m3fn, 7), "e5m2": (ml_dtypes.float8_e5m2, 14)}[fmt]
    v = np.moveaxis(np.asarray(x, np.float32).astype(ml_dtypes.bfloat16).astype(np.float64), axis, -1)
    blocks = v.reshape(v.shape[:-1] + (-1, 32))
    amax = np.abs(blocks).max(-1, keepdims=True)
    byte = np.maximum(np.where(amax > 0, np.frexp(amax)[1] - 1 + 127, 0) - down, 1)
    scale = np.exp2(byte - 127.0)
    codes = (blocks / scale).astype(np.float32).astype(dtype).astype(np.float64)
    return np.moveaxis((codes * scale).reshape(v.shape), -1, axis)


WIDE = False


def mx_kscale(k):
    if not WIDE:
        return np.ones(k)
    levels = np.array([10, -10, 5, -5, 0])
    if k % 512:
        return np.exp2(np.random.permutation(np.resize(levels, k // 32))).repeat(32)
    a = np.empty((k // 512, 16))
    for p in range(k // 512):
        a[p, :8] = np.random.permutation(np.resize(levels, 8))
        for g in range(8):
            far = levels[np.abs(levels - a[p, g]) >= 10]
            a[p, g + 8] = far[np.random.randint(len(far))]
    return np.exp2(a.ravel()).repeat(32)


def f64(x):
    return np.asarray(x).astype(np.float64)


def striped(idx):
    return np.tile(idx.reshape(-1, 16).T, (8, 1)).astype(np.uint16)


def unstriped(offs):
    return offs[:16].T.reshape(-1).astype(np.int64)


K, T, E, C, N = 512, 1024, 8, 256, 256


def by_expert(wq, xq):
    return np.concatenate([wq[e].T @ xq[:, e * C:(e + 1) * C] for e in range(E)], axis=1)


def setup_inputs():
    n = np.random.standard_normal
    s = mx_kscale(K)[:, None]
    first = np.random.permutation(np.repeat(np.arange(E), T // E))
    second = (first + 1 + np.random.permutation(np.repeat(np.arange(E - 1), -(-T // (E - 1)))[:T])) % E
    while np.bincount(second, minlength=E).max() != T // E:
        load = np.bincount(second, minlength=E); hi, lo = int(load.argmax()), int(load.argmin())
        t = np.flatnonzero((second == hi) & (first != lo))[0]; second[t] = lo
    slot_token = np.empty(E * C, np.int64); pos = np.empty((2, T), np.int64); fill = np.zeros(E, np.int64)
    place = np.stack([np.random.permutation(C) for _ in range(E)])
    for r, deal in enumerate((first, second)):
        for t in np.random.permutation(T):
            e = deal[t]; j = e * C + place[e, fill[e]]; fill[e] += 1; slot_token[j] = t; pos[r, t] = j
    g = np.random.uniform(0.2, 0.8, T)
    return {
        "xT": (n((K, T)) * s).astype(np.float32),
        "w": (n((E, K, N)) / np.sqrt(K) / s[None]).astype(np.float32),
        "gate": np.stack([np.tile(g, (N, 1)), np.tile(1.0 - g, (N, 1))]).astype(np.float32),
        "offs": striped(slot_token),
        "pos1": striped(pos[0]),
        "pos2": striped(pos[1]),
    }


def reference(xT, w, gate, offs, pos1, pos2):
    idx = unstriped(offs)
    xq = mxq(f64(xT)[:, idx], 0, "e4m3")
    y = by_expert(mxq(f64(w), 1, "e4m3"), xq)
    return f64(gate[0]) * y[:, unstriped(pos1)] + f64(gate[1]) * y[:, unstriped(pos2)]

@@ -1,0 +1,177 @@
+from contextlib import ExitStack
+
+import concourse.mybir as mybir
+
+K, T, E, C, N = 512, 1024, 8, 256, 256
+FLOPS = 2 * K * N * E * C
+
+F32 = mybir.dt.float32
+BF16 = mybir.dt.bfloat16
+U32 = mybir.dt.uint32
+U16 = mybir.dt.uint16
+U8 = mybir.dt.uint8
+FP8X4 = mybir.dt.float8_e4m3fn_x4
+MULT = mybir.AluOpType.mult
+ADD = mybir.AluOpType.add
+COPY = mybir.ActivationFunctionType.Copy
+
+P = 128
+PACK = 4
+BLOCKS = N // P
+HALF = 512
+
+S_EXPERTS = (6, 7)
+
+
+def tile_routed_moe_kernel(tc, xT, w, gate, offs, pos1, pos2, out):
+    nc = tc.nc
+    with ExitStack() as ctx:
+        lists = ctx.enter_context(tc.tile_pool(name="lists", bufs=1))
+        keep = ctx.enter_context(tc.tile_pool(name="keep", bufs=1))
+        ring = ctx.enter_context(tc.tile_pool(name="ring", bufs=2))
+        psum = ctx.enter_context(tc.psum_pool(name="psum", bufs=1))
+
+        offs_t = lists.tile([P, E * C // 16], U16, name="offs_t")
+        nc.sync.dma_start(offs_t[:], offs)
+        x_rows = xT.rearrange("(p t) n -> p t n", t=PACK)
+        x_raw = keep.tile([P, PACK, T], F32, name="x_raw")
+        for t in range(PACK):
+            nc.sync.dma_start(x_raw[:, t, :], x_rows[:, t, :])
+        pos_t = []
+        gate_t = {}
+        w_raw = []
+
+        def load_lists():
+            for r, pos in enumerate((pos1, pos2)):
+                lst = lists.tile([P, T // 16], U16, name="pos_t%d" % r)
+                nc.sync.dma_start(lst[:], pos)
+                pos_t.append(lst)
+
+        def load_gate(mb):
+            for r in range(2):
+                g = keep.tile([P, T], F32, name="gate_t%d_%d" % (r, mb))
+                nc.sync.dma_start(g[:], gate[r, mb * P:(mb + 1) * P, :])
+                gate_t[(r, mb)] = g
+
+        def load_w():
+            for e in range(E):
+                raw = keep.tile([P, PACK, N], F32, name="w_raw%d" % e)
+                nc.sync.dma_start(raw[:], w[e].rearrange("(p j) n -> p j n", j=PACK))
+                w_raw.append(raw)
+
+        load_lists()
+        load_gate(0)
+        load_w()
+        load_gate(1)
+
+        x_bf = keep.tile([P, PACK, T], BF16, name="x_bf")
+        x_codes = keep.tile([P, E * C], U32, name="x_codes", align_bytes=64)
+        x_scales = keep.tile([P, E * C], U8, name="x_scales", align_bytes=64)
+        w_codes = [keep.tile([P, E * P], U32, name="w_codes%d" % mb, align_bytes=64) for mb in range(BLOCKS)]
+        w_scales = [keep.tile([P, E * P], U8, name="w_scales%d" % mb, align_bytes=64) for mb in range(BLOCKS)]
+        y_sb = [keep.tile([P, E * C], F32, name="y_sb%d" % mb) for mb in range(BLOCKS)]
+        banks = {}
+        for mb in range(BLOCKS):
+            for b in range(E // 2):
+                banks[(mb, b)] = psum.tile([P, 2 * C], F32, name="bank%d_%d" % (mb, b))
+        x_grouped = [keep.tile([P, 2 * C, PACK], BF16, name="x_grp%d" % pair, align_bytes=64) for pair in range(E // 2)]
+        w_grouped = {}
+
+        def gather(e, t):
+            dst = x_grouped[e // 2][:, (e % 2) * C:(e % 2 + 1) * C, t]
+            slot_list = offs_t[:, e * (C // 16):(e + 1) * (C // 16)]
+            if e in S_EXPERTS:
+                nc.scalar.activation(dst, x_bf[:, t, :].indirect(slot_list), COPY)
+            else:
+                nc.vector.tensor_copy(dst, x_raw[:, t, :].indirect(slot_list))
+
+        def x_quantize(pair):
+            cols = slice(2 * pair * C, (2 * pair + 2) * C)
+            nc.vector.quantize_mx(
+                out=x_codes[:, cols].bitcast(FP8X4),
+                scales=x_scales[:, cols],
+                in_=x_grouped[pair][:].rearrange("p n t -> p (n t)"),
+            )
+
+        def w_interleave(engine, mb):
+            grp = ring.tile([P, E, P, PACK], BF16, name="w_grp", bufs=1, align_bytes=64)
+            for e in range(E):
+                src = w_raw[e][:, :, mb * P:(mb + 1) * P].rearrange("p j n -> p n j")
+                if engine == "vector":
+                    nc.vector.tensor_copy(grp[:, e, :, :], src)
+                else:
+                    nc.scalar.copy(grp[:, e, :, :], src)
+            w_grouped[mb] = grp
+
+        def w_quantize(mb):
+            nc.vector.quantize_mx(
+                out=w_codes[mb][:].bitcast(FP8X4),
+                scales=w_scales[mb][:],
+                in_=w_grouped[mb][:].rearrange("p i n j -> p (i n j)"),
+            )
+
+        def multiply(pair, mb):
+            for e in (2 * pair, 2 * pair + 1):
+                nc.tensor.matmul_mx(
+                    out=banks[(mb, pair)][:, (e % 2) * C:(e % 2 + 1) * C],
+                    lhsT=w_codes[mb][:, e * P:(e + 1) * P].bitcast(FP8X4),
+                    lhsT_scale=w_scales[mb][:, e * P:(e + 1) * P],
+                    rhs=x_codes[:, e * C:(e + 1) * C].bitcast(FP8X4),
+                    rhs_scale=x_scales[:, e * C:(e + 1) * C],
+                    start=True,
+                    stop=True,
+                )
+
+        def empty(engine, pair, mb):
+            dst = y_sb[mb][:, 2 * pair * C:(2 * pair + 2) * C]
+            if engine == "vector":
+                nc.vector.tensor_copy(dst, banks[(mb, pair)][:])
+            else:
+                nc.scalar.copy(dst, banks[(mb, pair)][:])
+
+        def combine(mb, first, count):
+            prods = []
+            for r in range(2):
+                prod = ring.tile([P, count], F32, name="prod%d_%d" % (r, count))
+                nc.vector.tensor_tensor(
+                    prod[:],
+                    y_sb[mb][:].indirect(pos_t[r][:, first // 16:(first + count) // 16]),
+                    gate_t[(r, mb)][:, first:first + count],
+                    MULT,
+                )
+                prods.append(prod)
+            res = ring.tile([P, count], F32, name="res%d" % count)
+            nc.vector.tensor_tensor(res[:], prods[0][:], prods[1][:], ADD)
+            nc.sync.dma_start(out[mb * P:(mb + 1) * P, first:first + count], res[:])
+
+        for t in range(PACK):
+            nc.scalar.copy(x_bf[:, t, :], x_raw[:, t, :])
+        for t in range(PACK):
+            gather(0, t)
+            gather(1, t)
+        for e in S_EXPERTS:
+            for t in range(PACK):
+                gather(e, t)
+        w_interleave("scalar", 0)
+        w_quantize(0)
+        x_quantize(3)
+        for pair in (1, 2):
+            for t in range(PACK):
+                gather(2 * pair, t)
+                gather(2 * pair + 1, t)
+                if t == 0:
+                    x_quantize(pair - 1)
+        x_quantize(2)
+        for pair in range(E // 2):
+            multiply(pair, 0)
+            empty("scalar", pair, 0)
+
+        w_interleave("vector", 1)
+        w_quantize(1)
+        for pair in range(E // 2):
+            multiply(pair, 1)
+            empty("scalar", pair, 1)
+
+        for mb in range(BLOCKS):
+            combine(mb, 0, T // 2)
+            combine(mb, T // 2, T // 2)

@@ -13,14 +13,12 @@ U8 = mybir.dt.uint8
 FP8X4 = mybir.dt.float8_e4m3fn_x4
 MULT = mybir.AluOpType.mult
 ADD = mybir.AluOpType.add
-COPY = mybir.ActivationFunctionType.Copy
 
 P = 128
 PACK = 4
 BLOCKS = N // P
-HALF = 512
-
-S_EXPERTS = (6, 7)
+CHUNK = 512
+CHUNKS = E * C // CHUNK
 
 
 def tile_routed_moe_kernel(tc, xT, w, gate, offs, pos1, pos2, out):
@@ -34,86 +32,79 @@ def tile_routed_moe_kernel(tc, xT, w, gate, offs, pos1, pos2, out):
         offs_t = lists.tile([P, E * C // 16], U16, name="offs_t")
         nc.sync.dma_start(offs_t[:], offs)
         x_rows = xT.rearrange("(p t) n -> p t n", t=PACK)
-        x_raw = keep.tile([P, PACK, T], F32, name="x_raw")
-        for t in range(PACK):
-            nc.sync.dma_start(x_raw[:, t, :], x_rows[:, t, :])
+        x_plane = {}
+        w_raw = {}
+        for kind, i in (("x", 0), ("w", 0), ("w", 1), ("x", 1), ("w", 2), ("w", 3), ("x", 2), ("w", 4), ("w", 5), ("w", 6), ("x", 3), ("w", 7)):
+            if kind == "x":
+                x_plane[i] = keep.tile([P, T], F32, name="x_plane%d" % i)
+                nc.sync.dma_start(x_plane[i][:], x_rows[:, i, :])
+            else:
+                w_raw[i] = keep.tile([P, PACK, N], F32, name="w_raw%d" % i)
+                nc.sync.dma_start(w_raw[i][:], w[i].rearrange("(p j) n -> p j n", j=PACK))
         pos_t = []
+        for r, pos in enumerate((pos1, pos2)):
+            lst = lists.tile([P, T // 16], U16, name="pos_t%d" % r)
+            nc.sync.dma_start(lst[:], pos)
+            pos_t.append(lst)
         gate_t = {}
-        w_raw = []
-
-        def load_lists():
-            for r, pos in enumerate((pos1, pos2)):
-                lst = lists.tile([P, T // 16], U16, name="pos_t%d" % r)
-                nc.sync.dma_start(lst[:], pos)
-                pos_t.append(lst)
-
-        def load_gate(mb):
+        for mb in range(BLOCKS):
             for r in range(2):
                 g = keep.tile([P, T], F32, name="gate_t%d_%d" % (r, mb))
                 nc.sync.dma_start(g[:], gate[r, mb * P:(mb + 1) * P, :])
                 gate_t[(r, mb)] = g
 
-        def load_w():
-            for e in range(E):
-                raw = keep.tile([P, PACK, N], F32, name="w_raw%d" % e)
-                nc.sync.dma_start(raw[:], w[e].rearrange("(p j) n -> p j n", j=PACK))
-                w_raw.append(raw)
-
-        load_lists()
-        load_gate(0)
-        load_w()
-        load_gate(1)
-
-        x_bf = keep.tile([P, PACK, T], BF16, name="x_bf")
         x_codes = keep.tile([P, E * C], U32, name="x_codes", align_bytes=64)
         x_scales = keep.tile([P, E * C], U8, name="x_scales", align_bytes=64)
+        w_grouped = keep.tile([P, BLOCKS, E, P, PACK], BF16, name="w_grouped", align_bytes=64)
         w_codes = [keep.tile([P, E * P], U32, name="w_codes%d" % mb, align_bytes=64) for mb in range(BLOCKS)]
         w_scales = [keep.tile([P, E * P], U8, name="w_scales%d" % mb, align_bytes=64) for mb in range(BLOCKS)]
         y_sb = [keep.tile([P, E * C], F32, name="y_sb%d" % mb) for mb in range(BLOCKS)]
         banks = {}
         for mb in range(BLOCKS):
-            for b in range(E // 2):
-                banks[(mb, b)] = psum.tile([P, 2 * C], F32, name="bank%d_%d" % (mb, b))
-        x_grouped = [keep.tile([P, 2 * C, PACK], BF16, name="x_grp%d" % pair, align_bytes=64) for pair in range(E // 2)]
-        w_grouped = {}
+            for b in range(CHUNKS):
+                banks[(mb, b)] = psum.tile([P, CHUNK], F32, name="bank%d_%d" % (mb, b))
+        gathered = {}
+        x_grouped = {}
 
-        def gather(e, t):
-            dst = x_grouped[e // 2][:, (e % 2) * C:(e % 2 + 1) * C, t]
-            slot_list = offs_t[:, e * (C // 16):(e + 1) * (C // 16)]
-            if e in S_EXPERTS:
-                nc.scalar.activation(dst, x_bf[:, t, :].indirect(slot_list), COPY)
-            else:
-                nc.vector.tensor_copy(dst, x_raw[:, t, :].indirect(slot_list))
+        def gather(c):
+            g4 = ring.tile([P, PACK, CHUNK], F32, name="g4", bufs=3)
+            slot_list = offs_t[:, c * (CHUNK // 16):(c + 1) * (CHUNK // 16)]
+            for t in range(PACK):
+                nc.vector.tensor_copy(g4[:, t, :], x_plane[t][:].indirect(slot_list))
+            gathered[c] = g4
 
-        def x_quantize(pair):
-            cols = slice(2 * pair * C, (2 * pair + 2) * C)
+        def x_interleave(c):
+            grp = keep.tile([P, CHUNK, PACK], BF16, name="x_grp%d" % c, align_bytes=64)
+            nc.scalar.copy(grp[:], gathered[c][:].rearrange("p t n -> p n t"))
+            x_grouped[c] = grp
+
+        def x_quantize(c):
+            cols = slice(c * CHUNK, (c + 1) * CHUNK)
             nc.vector.quantize_mx(
                 out=x_codes[:, cols].bitcast(FP8X4),
                 scales=x_scales[:, cols],
-                in_=x_grouped[pair][:].rearrange("p n t -> p (n t)"),
+                in_=x_grouped[c][:].rearrange("p n t -> p (n t)"),
             )
 
-        def w_interleave(engine, mb):
-            grp = ring.tile([P, E, P, PACK], BF16, name="w_grp", bufs=1, align_bytes=64)
-            for e in range(E):
-                src = w_raw[e][:, :, mb * P:(mb + 1) * P].rearrange("p j n -> p n j")
-                if engine == "vector":
-                    nc.vector.tensor_copy(grp[:, e, :, :], src)
-                else:
-                    nc.scalar.copy(grp[:, e, :, :], src)
-            w_grouped[mb] = grp
+        def w_interleave(engine, e):
+            dst = w_grouped[:, :, e, :, :]
+            src = w_raw[e][:].rearrange("p j (m n) -> p m n j", m=BLOCKS)
+            if engine == "vector":
+                nc.vector.tensor_copy(dst, src)
+            else:
+                nc.scalar.copy(dst, src)
 
         def w_quantize(mb):
             nc.vector.quantize_mx(
                 out=w_codes[mb][:].bitcast(FP8X4),
                 scales=w_scales[mb][:],
-                in_=w_grouped[mb][:].rearrange("p i n j -> p (i n j)"),
+                in_=w_grouped[:, mb, :, :, :].rearrange("p e n j -> p (e n j)"),
             )
 
-        def multiply(pair, mb):
-            for e in (2 * pair, 2 * pair + 1):
+        def multiply(c, mb):
+            for e in (2 * c, 2 * c + 1):
                 nc.tensor.matmul_mx(
-                    out=banks[(mb, pair)][:, (e % 2) * C:(e % 2 + 1) * C],
+                    out=banks[(mb, c)][:, (e % 2) * C:(e % 2 + 1) * C],
                     lhsT=w_codes[mb][:, e * P:(e + 1) * P].bitcast(FP8X4),
                     lhsT_scale=w_scales[mb][:, e * P:(e + 1) * P],
                     rhs=x_codes[:, e * C:(e + 1) * C].bitcast(FP8X4),
@@ -121,13 +112,7 @@ def tile_routed_moe_kernel(tc, xT, w, gate, offs, pos1, pos2, out):
                     start=True,
                     stop=True,
                 )
-
-        def empty(engine, pair, mb):
-            dst = y_sb[mb][:, 2 * pair * C:(2 * pair + 2) * C]
-            if engine == "vector":
-                nc.vector.tensor_copy(dst, banks[(mb, pair)][:])
-            else:
-                nc.scalar.copy(dst, banks[(mb, pair)][:])
+            nc.scalar.copy(y_sb[mb][:, c * CHUNK:(c + 1) * CHUNK], banks[(mb, c)][:])
 
         def combine(mb, first, count):
             prods = []
@@ -144,34 +129,19 @@ def tile_routed_moe_kernel(tc, xT, w, gate, offs, pos1, pos2, out):
             nc.vector.tensor_tensor(res[:], prods[0][:], prods[1][:], ADD)
             nc.sync.dma_start(out[mb * P:(mb + 1) * P, first:first + count], res[:])
 
-        for t in range(PACK):
-            nc.scalar.copy(x_bf[:, t, :], x_raw[:, t, :])
-        for t in range(PACK):
-            gather(0, t)
-            gather(1, t)
-        for e in S_EXPERTS:
-            for t in range(PACK):
-                gather(e, t)
-        w_interleave("scalar", 0)
+        for e in range(E - 1):
+            w_interleave("scalar", e)
+        for c in range(CHUNKS):
+            gather(c)
+            x_interleave(c)
+            x_quantize(c)
+        w_interleave("vector", E - 1)
         w_quantize(0)
-        x_quantize(3)
-        for pair in (1, 2):
-            for t in range(PACK):
-                gather(2 * pair, t)
-                gather(2 * pair + 1, t)
-                if t == 0:
-                    x_quantize(pair - 1)
-        x_quantize(2)
-        for pair in range(E // 2):
-            multiply(pair, 0)
-            empty("scalar", pair, 0)
-
-        w_interleave("vector", 1)
+        for c in range(CHUNKS):
+            multiply(c, 0)
         w_quantize(1)
-        for pair in range(E // 2):
-            multiply(pair, 1)
-            empty("scalar", pair, 1)
-
+        for c in range(CHUNKS):
+            multiply(c, 1)
         for mb in range(BLOCKS):
             combine(mb, 0, T // 2)
             combine(mb, T // 2, T // 2)

@@ -20,6 +20,11 @@ BLOCKS = N // P
 CHUNK = 512
 CHUNKS = E * C // CHUNK
 
+LOAD_ORDER = (
+    ("x", 0), ("w", 0), ("w", 1), ("x", 1), ("w", 2), ("w", 3), ("x", 2), ("w", 4), ("w", 5), ("w", 6), ("x", 3),
+    ("pos", 0), ("pos", 1), ("gate", 0), ("w", 7), ("gate", 1),
+)
+
 
 def tile_routed_moe_kernel(tc, xT, w, gate, offs, pos1, pos2, out):
     nc = tc.nc
@@ -34,49 +39,48 @@ def tile_routed_moe_kernel(tc, xT, w, gate, offs, pos1, pos2, out):
         x_rows = xT.rearrange("(p t) n -> p t n", t=PACK)
         x_plane = {}
         w_raw = {}
-        for kind, i in (("x", 0), ("w", 0), ("w", 1), ("x", 1), ("w", 2), ("w", 3), ("x", 2), ("w", 4), ("w", 5), ("w", 6), ("x", 3), ("w", 7)):
+        pos_t = {}
+        gate_t = {}
+        for kind, i in LOAD_ORDER:
             if kind == "x":
                 x_plane[i] = keep.tile([P, T], F32, name="x_plane%d" % i)
                 nc.sync.dma_start(x_plane[i][:], x_rows[:, i, :])
-            else:
+            elif kind == "w":
                 w_raw[i] = keep.tile([P, PACK, N], F32, name="w_raw%d" % i)
                 nc.sync.dma_start(w_raw[i][:], w[i].rearrange("(p j) n -> p j n", j=PACK))
-        pos_t = []
-        for r, pos in enumerate((pos1, pos2)):
-            lst = lists.tile([P, T // 16], U16, name="pos_t%d" % r)
-            nc.sync.dma_start(lst[:], pos)
-            pos_t.append(lst)
-        gate_t = {}
-        for mb in range(BLOCKS):
-            for r in range(2):
-                g = keep.tile([P, T], F32, name="gate_t%d_%d" % (r, mb))
-                nc.sync.dma_start(g[:], gate[r, mb * P:(mb + 1) * P, :])
-                gate_t[(r, mb)] = g
+            elif kind == "pos":
+                pos_t[i] = lists.tile([P, T // 16], U16, name="pos_t%d" % i)
+                nc.sync.dma_start(pos_t[i][:], (pos1, pos2)[i])
+            else:
+                for r in range(2):
+                    gate_t[(r, i)] = keep.tile([P, T], F32, name="gate_t%d_%d" % (r, i))
+                    nc.sync.dma_start(gate_t[(r, i)][:], gate[r, i * P:(i + 1) * P, :])
 
         x_codes = keep.tile([P, E * C], U32, name="x_codes", align_bytes=64)
         x_scales = keep.tile([P, E * C], U8, name="x_scales", align_bytes=64)
         w_grouped = keep.tile([P, BLOCKS, E, P, PACK], BF16, name="w_grouped", align_bytes=64)
-        w_codes = [keep.tile([P, E * P], U32, name="w_codes%d" % mb, align_bytes=64) for mb in range(BLOCKS)]
+        w_codes = {0: keep.tile([P, E * P], U32, name="w_codes0", align_bytes=64)}
         w_scales = [keep.tile([P, E * P], U8, name="w_scales%d" % mb, align_bytes=64) for mb in range(BLOCKS)]
         y_sb = [keep.tile([P, E * C], F32, name="y_sb%d" % mb) for mb in range(BLOCKS)]
         banks = {}
         for mb in range(BLOCKS):
-            for b in range(CHUNKS):
-                banks[(mb, b)] = psum.tile([P, CHUNK], F32, name="bank%d_%d" % (mb, b))
+            for c in range(CHUNKS):
+                banks[(mb, c)] = psum.tile([P, CHUNK], F32, name="bank%d_%d" % (mb, c))
         gathered = {}
         x_grouped = {}
 
         def gather(c):
-            g4 = ring.tile([P, PACK, CHUNK], F32, name="g4", bufs=3)
+            gathered[c] = ring.tile([P, PACK, CHUNK], F32, name="g4", bufs=3)
             slot_list = offs_t[:, c * (CHUNK // 16):(c + 1) * (CHUNK // 16)]
             for t in range(PACK):
-                nc.vector.tensor_copy(g4[:, t, :], x_plane[t][:].indirect(slot_list))
-            gathered[c] = g4
+                nc.vector.tensor_copy(gathered[c][:, t, :], x_plane[t][:].indirect(slot_list))
 
         def x_interleave(c):
-            grp = keep.tile([P, CHUNK, PACK], BF16, name="x_grp%d" % c, align_bytes=64)
-            nc.scalar.copy(grp[:], gathered[c][:].rearrange("p t n -> p n t"))
-            x_grouped[c] = grp
+            if c < CHUNKS - 1:
+                x_grouped[c] = keep.tile([P, CHUNK, PACK], BF16, name="x_grp%d" % c, align_bytes=64)
+            else:
+                x_grouped[c] = ring.tile([P, CHUNK, PACK], BF16, name="turn", bufs=1, align_bytes=64)
+            nc.scalar.copy(x_grouped[c][:], gathered[c][:].rearrange("p t n -> p n t"))
 
         def x_quantize(c):
             cols = slice(c * CHUNK, (c + 1) * CHUNK)
@@ -86,15 +90,12 @@ def tile_routed_moe_kernel(tc, xT, w, gate, offs, pos1, pos2, out):
                 in_=x_grouped[c][:].rearrange("p n t -> p (n t)"),
             )
 
-        def w_interleave(engine, e):
-            dst = w_grouped[:, :, e, :, :]
-            src = w_raw[e][:].rearrange("p j (m n) -> p m n j", m=BLOCKS)
-            if engine == "vector":
-                nc.vector.tensor_copy(dst, src)
-            else:
-                nc.scalar.copy(dst, src)
+        def w_interleave(copy, e):
+            copy(w_grouped[:, :, e, :, :], w_raw[e][:].rearrange("p j (m n) -> p m n j", m=BLOCKS))
 
         def w_quantize(mb):
+            if mb == 1:
+                w_codes[mb] = ring.tile([P, E * P], U32, name="turn", bufs=1, align_bytes=64)
             nc.vector.quantize_mx(
                 out=w_codes[mb][:].bitcast(FP8X4),
                 scales=w_scales[mb][:],
@@ -130,18 +131,21 @@ def tile_routed_moe_kernel(tc, xT, w, gate, offs, pos1, pos2, out):
             nc.sync.dma_start(out[mb * P:(mb + 1) * P, first:first + count], res[:])
 
         for e in range(E - 1):
-            w_interleave("scalar", e)
+            w_interleave(nc.scalar.copy, e)
         for c in range(CHUNKS):
             gather(c)
             x_interleave(c)
-            x_quantize(c)
-        w_interleave("vector", E - 1)
+        x_quantize(0)
+        w_interleave(nc.vector.tensor_copy, E - 1)
         w_quantize(0)
-        for c in range(CHUNKS):
+        multiply(0, 0)
+        for c in range(1, CHUNKS):
+            x_quantize(c)
             multiply(c, 0)
         w_quantize(1)
         for c in range(CHUNKS):
             multiply(c, 1)
-        for mb in range(BLOCKS):
-            combine(mb, 0, T // 2)
-            combine(mb, T // 2, T // 2)
+        combine(0, 0, T)
+        combine(1, 0, T // 2)
+        combine(1, T // 2, T // 4)
+        combine(1, 3 * T // 4, T // 4)

@@ -21,8 +21,8 @@ CHUNK = 512
 CHUNKS = E * C // CHUNK
 
 LOAD_ORDER = (
-    ("x", 0), ("w", 0), ("w", 1), ("x", 1), ("w", 2), ("w", 3), ("x", 2), ("w", 4), ("w", 5), ("w", 6), ("x", 3),
-    ("pos", 0), ("pos", 1), ("gate", 0), ("w", 7), ("gate", 1),
+    ("x", 0), ("w", 0), ("x", 1), ("w", 1), ("w", 2), ("x", 2), ("w", 3), ("w", 4), ("w", 5), ("w", 6), ("x", 3),
+    ("pos", 0), ("pos", 1), ("gate", (0, 0)), ("w", 7), ("gate", (1, 0)), ("gate", (0, 1)), ("gate", (1, 1)),
 )
 
 
@@ -52,9 +52,9 @@ def tile_routed_moe_kernel(tc, xT, w, gate, offs, pos1, pos2, out):
                 pos_t[i] = lists.tile([P, T // 16], U16, name="pos_t%d" % i)
                 nc.sync.dma_start(pos_t[i][:], (pos1, pos2)[i])
             else:
-                for r in range(2):
-                    gate_t[(r, i)] = keep.tile([P, T], F32, name="gate_t%d_%d" % (r, i))
-                    nc.sync.dma_start(gate_t[(r, i)][:], gate[r, i * P:(i + 1) * P, :])
+                r, mb = i
+                gate_t[i] = keep.tile([P, T], F32, name="gate_t%d_%d" % i)
+                nc.sync.dma_start(gate_t[i][:], gate[r, mb * P:(mb + 1) * P, :])
 
         x_codes = keep.tile([P, E * C], U32, name="x_codes", align_bytes=64)
         x_scales = keep.tile([P, E * C], U8, name="x_scales", align_bytes=64)
@@ -80,7 +80,10 @@ def tile_routed_moe_kernel(tc, xT, w, gate, offs, pos1, pos2, out):
                 x_grouped[c] = keep.tile([P, CHUNK, PACK], BF16, name="x_grp%d" % c, align_bytes=64)
             else:
                 x_grouped[c] = ring.tile([P, CHUNK, PACK], BF16, name="turn", bufs=1, align_bytes=64)
-            nc.scalar.copy(x_grouped[c][:], gathered[c][:].rearrange("p t n -> p n t"))
+            nc.scalar.copy(
+                x_grouped[c][:].rearrange("p (g i) t -> p g t i", i=4),
+                gathered[c][:].rearrange("p t (g i) -> p g t i", i=4),
+            )
 
         def x_quantize(c):
             cols = slice(c * CHUNK, (c + 1) * CHUNK)
@@ -135,11 +138,9 @@ def tile_routed_moe_kernel(tc, xT, w, gate, offs, pos1, pos2, out):
         for c in range(CHUNKS):
             gather(c)
             x_interleave(c)
-        x_quantize(0)
         w_interleave(nc.vector.tensor_copy, E - 1)
         w_quantize(0)
-        multiply(0, 0)
-        for c in range(1, CHUNKS):
+        for c in range(CHUNKS):
             x_quantize(c)
             multiply(c, 0)
         w_quantize(1)

@@ -21,7 +21,7 @@ CHUNK = 512
 CHUNKS = E * C // CHUNK
 
 LOAD_ORDER = (
-    ("x", 0), ("w", 0), ("x", 1), ("w", 1), ("w", 2), ("x", 2), ("w", 3), ("w", 4), ("w", 5), ("w", 6), ("x", 3),
+    ("x", 0), ("offs", 0), ("w", 0), ("x", 1), ("w", 1), ("w", 2), ("x", 2), ("w", 3), ("w", 4), ("w", 5), ("w", 6), ("x", 3),
     ("pos", 0), ("pos", 1), ("gate", (0, 0)), ("w", 7), ("gate", (1, 0)), ("gate", (0, 1)), ("gate", (1, 1)),
 )
 
@@ -35,7 +35,6 @@ def tile_routed_moe_kernel(tc, xT, w, gate, offs, pos1, pos2, out):
         psum = ctx.enter_context(tc.psum_pool(name="psum", bufs=1))
 
         offs_t = lists.tile([P, E * C // 16], U16, name="offs_t")
-        nc.sync.dma_start(offs_t[:], offs)
         x_rows = xT.rearrange("(p t) n -> p t n", t=PACK)
         x_plane = {}
         w_raw = {}
@@ -48,6 +47,8 @@ def tile_routed_moe_kernel(tc, xT, w, gate, offs, pos1, pos2, out):
             elif kind == "w":
                 w_raw[i] = keep.tile([P, PACK, N], F32, name="w_raw%d" % i)
                 nc.sync.dma_start(w_raw[i][:], w[i].rearrange("(p j) n -> p j n", j=PACK))
+            elif kind == "offs":
+                nc.sync.dma_start(offs_t[:], offs)
             elif kind == "pos":
                 pos_t[i] = lists.tile([P, T // 16], U16, name="pos_t%d" % i)
                 nc.sync.dma_start(pos_t[i][:], (pos1, pos2)[i])
@@ -139,14 +140,15 @@ def tile_routed_moe_kernel(tc, xT, w, gate, offs, pos1, pos2, out):
             gather(c)
             x_interleave(c)
         w_interleave(nc.vector.tensor_copy, E - 1)
+        x_quantize(0)
         w_quantize(0)
-        for c in range(CHUNKS):
+        multiply(0, 0)
+        for c in range(1, CHUNKS):
             x_quantize(c)
             multiply(c, 0)
         w_quantize(1)
         for c in range(CHUNKS):
             multiply(c, 1)
         combine(0, 0, T)
-        combine(1, 0, T // 2)
-        combine(1, T // 2, T // 4)
+        combine(1, 0, 3 * T // 4)
         combine(1, 3 * T // 4, T // 4)

@@ -13,17 +13,15 @@ U8 = mybir.dt.uint8
 FP8X4 = mybir.dt.float8_e4m3fn_x4
 MULT = mybir.AluOpType.mult
 ADD = mybir.AluOpType.add
+COPY = mybir.ActivationFunctionType.Copy
 
 P = 128
 PACK = 4
 BLOCKS = N // P
 CHUNK = 512
 CHUNKS = E * C // CHUNK
-
-LOAD_ORDER = (
-    ("x", 0), ("offs", 0), ("w", 0), ("x", 1), ("w", 1), ("w", 2), ("x", 2), ("w", 3), ("w", 4), ("w", 5), ("w", 6), ("x", 3),
-    ("pos", 0), ("pos", 1), ("gate", (0, 0)), ("w", 7), ("gate", (1, 0)), ("gate", (0, 1)), ("gate", (1, 1)),
-)
+V_CHUNKS = 2
+HALF = E // 2
 
 
 def tile_routed_moe_kernel(tc, xT, w, gate, offs, pos1, pos2, out):
@@ -36,31 +34,29 @@ def tile_routed_moe_kernel(tc, xT, w, gate, offs, pos1, pos2, out):
 
         offs_t = lists.tile([P, E * C // 16], U16, name="offs_t")
         x_rows = xT.rearrange("(p t) n -> p t n", t=PACK)
-        x_plane = {}
-        w_raw = {}
-        pos_t = {}
+        x_plane = [keep.tile([P, T], F32, name="x_plane%d" % t) for t in range(PACK)]
+        w_raw = [keep.tile([P, PACK, N], F32, name="w_raw%d" % e) for e in range(E - 1)]
+        w_raw.append(ring.tile([P, PACK, N], F32, name="turn", bufs=1, align_bytes=64))
+        pos_t = [lists.tile([P, T // 16], U16, name="pos_t%d" % r) for r in range(2)]
         gate_t = {}
-        for kind, i in LOAD_ORDER:
-            if kind == "x":
-                x_plane[i] = keep.tile([P, T], F32, name="x_plane%d" % i)
-                nc.sync.dma_start(x_plane[i][:], x_rows[:, i, :])
-            elif kind == "w":
-                w_raw[i] = keep.tile([P, PACK, N], F32, name="w_raw%d" % i)
-                nc.sync.dma_start(w_raw[i][:], w[i].rearrange("(p j) n -> p j n", j=PACK))
-            elif kind == "offs":
-                nc.sync.dma_start(offs_t[:], offs)
-            elif kind == "pos":
-                pos_t[i] = lists.tile([P, T // 16], U16, name="pos_t%d" % i)
-                nc.sync.dma_start(pos_t[i][:], (pos1, pos2)[i])
-            else:
-                r, mb = i
-                gate_t[i] = keep.tile([P, T], F32, name="gate_t%d_%d" % i)
-                nc.sync.dma_start(gate_t[i][:], gate[r, mb * P:(mb + 1) * P, :])
+        nc.sync.dma_start(x_plane[0][:], x_rows[:, 0, :])
+        nc.sync.dma_start(offs_t[:], offs)
+        for t in range(1, PACK):
+            nc.sync.dma_start(x_plane[t][:], x_rows[:, t, :])
+        for e in range(E):
+            nc.sync.dma_start(w_raw[e][:], w[e].rearrange("(p j) n -> p j n", j=PACK))
+        for r in range(2):
+            nc.sync.dma_start(pos_t[r][:], (pos1, pos2)[r])
+        for mb in range(BLOCKS):
+            for r in range(2):
+                gate_t[(r, mb)] = keep.tile([P, T], F32, name="gate_t%d_%d" % (r, mb))
+                nc.sync.dma_start(gate_t[(r, mb)][:], gate[r, mb * P:(mb + 1) * P, :])
 
+        x_bf = [keep.tile([P, T], BF16, name="x_bf%d" % t) for t in range(PACK)]
         x_codes = keep.tile([P, E * C], U32, name="x_codes", align_bytes=64)
-        x_scales = keep.tile([P, E * C], U8, name="x_scales", align_bytes=64)
+        x_scales = ring.tile([P, E * C], U8, name="turn", bufs=1, align_bytes=64)
         w_grouped = keep.tile([P, BLOCKS, E, P, PACK], BF16, name="w_grouped", align_bytes=64)
-        w_codes = {0: keep.tile([P, E * P], U32, name="w_codes0", align_bytes=64)}
+        w_codes = [keep.tile([P, E * P], U32, name="w_codes%d" % mb, align_bytes=64) for mb in range(BLOCKS)]
         w_scales = [keep.tile([P, E * P], U8, name="w_scales%d" % mb, align_bytes=64) for mb in range(BLOCKS)]
         y_sb = [keep.tile([P, E * C], F32, name="y_sb%d" % mb) for mb in range(BLOCKS)]
         banks = {}
@@ -70,40 +66,45 @@ def tile_routed_moe_kernel(tc, xT, w, gate, offs, pos1, pos2, out):
         gathered = {}
         x_grouped = {}
 
+        def cast(t):
+            nc.vector.tensor_copy(x_bf[t][:], x_plane[t][:])
+
         def gather(c):
-            gathered[c] = ring.tile([P, PACK, CHUNK], F32, name="g4", bufs=3)
+            gathered[c] = ring.tile([P, PACK, CHUNK], F32, name="g4")
             slot_list = offs_t[:, c * (CHUNK // 16):(c + 1) * (CHUNK // 16)]
             for t in range(PACK):
                 nc.vector.tensor_copy(gathered[c][:, t, :], x_plane[t][:].indirect(slot_list))
 
         def x_interleave(c):
-            if c < CHUNKS - 1:
-                x_grouped[c] = keep.tile([P, CHUNK, PACK], BF16, name="x_grp%d" % c, align_bytes=64)
-            else:
-                x_grouped[c] = ring.tile([P, CHUNK, PACK], BF16, name="turn", bufs=1, align_bytes=64)
+            x_grouped[c] = keep.tile([P, CHUNK, PACK], BF16, name="x_grp%d" % c, align_bytes=64)
             nc.scalar.copy(
                 x_grouped[c][:].rearrange("p (g i) t -> p g t i", i=4),
                 gathered[c][:].rearrange("p t (g i) -> p g t i", i=4),
             )
 
-        def x_quantize(c):
-            cols = slice(c * CHUNK, (c + 1) * CHUNK)
+        def scalar_gather(e):
+            x_grouped[("s", e)] = keep.tile([P, C, PACK], BF16, name="x_grs%d" % e, align_bytes=64)
+            slot_list = offs_t[:, e * (C // 16):(e + 1) * (C // 16)]
+            for t in range(PACK):
+                nc.scalar.activation(x_grouped[("s", e)][:, :, t], x_bf[t][:].indirect(slot_list), COPY)
+
+        def x_quantize(key, first, count):
+            cols = slice(first, first + count)
             nc.vector.quantize_mx(
                 out=x_codes[:, cols].bitcast(FP8X4),
                 scales=x_scales[:, cols],
-                in_=x_grouped[c][:].rearrange("p n t -> p (n t)"),
+                in_=x_grouped[key][:].rearrange("p n t -> p (n t)"),
             )
 
         def w_interleave(copy, e):
             copy(w_grouped[:, :, e, :, :], w_raw[e][:].rearrange("p j (m n) -> p m n j", m=BLOCKS))
 
-        def w_quantize(mb):
-            if mb == 1:
-                w_codes[mb] = ring.tile([P, E * P], U32, name="turn", bufs=1, align_bytes=64)
+        def w_quantize(mb, h):
+            cols = slice(h * HALF * P, (h + 1) * HALF * P)
             nc.vector.quantize_mx(
-                out=w_codes[mb][:].bitcast(FP8X4),
-                scales=w_scales[mb][:],
-                in_=w_grouped[:, mb, :, :, :].rearrange("p e n j -> p (e n j)"),
+                out=w_codes[mb][:, cols].bitcast(FP8X4),
+                scales=w_scales[mb][:, cols],
+                in_=w_grouped[:, mb, h * HALF:(h + 1) * HALF, :, :].rearrange("p e n j -> p (e n j)"),
             )
 
         def multiply(c, mb):
@@ -134,19 +135,31 @@ def tile_routed_moe_kernel(tc, xT, w, gate, offs, pos1, pos2, out):
             nc.vector.tensor_tensor(res[:], prods[0][:], prods[1][:], ADD)
             nc.sync.dma_start(out[mb * P:(mb + 1) * P, first:first + count], res[:])
 
-        for e in range(E - 1):
-            w_interleave(nc.scalar.copy, e)
-        for c in range(CHUNKS):
+        warm = keep.tile([P, 2], F32, name="warm")
+        nc.vector.memset(warm[:, 0:1], 0.0)
+        nc.scalar.activation(warm[:, 1:2], warm[:, 0:1], COPY)
+
+        for t in range(PACK):
+            cast(t)
+        w_interleave(nc.scalar.copy, 0)
+        for c in range(V_CHUNKS):
             gather(c)
             x_interleave(c)
-        w_interleave(nc.vector.tensor_copy, E - 1)
-        x_quantize(0)
-        w_quantize(0)
-        multiply(0, 0)
-        for c in range(1, CHUNKS):
-            x_quantize(c)
+        for e in range(2 * V_CHUNKS, E):
+            scalar_gather(e)
+        for e in range(1, E):
+            w_interleave(nc.vector.tensor_copy, e)
+        for h in range(2):
+            w_quantize(0, h)
+        for c in range(V_CHUNKS):
+            x_quantize(c, c * CHUNK, CHUNK)
             multiply(c, 0)
-        w_quantize(1)
+        for c in range(V_CHUNKS, CHUNKS):
+            for e in (2 * c, 2 * c + 1):
+                x_quantize(("s", e), e * C, C)
+            multiply(c, 0)
+        for h in range(2):
+            w_quantize(1, h)
         for c in range(CHUNKS):
             multiply(c, 1)
         combine(0, 0, T)

@@ -22,6 +22,7 @@ CHUNK = 512
 CHUNKS = E * C // CHUNK
 V_CHUNKS = 2
 HALF = E // 2
+G_EXPERTS = 3
 
 
 def tile_routed_moe_kernel(tc, xT, w, gate, offs, pos1, pos2, out):
@@ -141,13 +142,14 @@ def tile_routed_moe_kernel(tc, xT, w, gate, offs, pos1, pos2, out):
 
         for t in range(PACK):
             cast(t)
-        w_interleave(nc.scalar.copy, 0)
+        for e in range(G_EXPERTS):
+            w_interleave(nc.gpsimd.tensor_copy, e)
         for c in range(V_CHUNKS):
             gather(c)
             x_interleave(c)
         for e in range(2 * V_CHUNKS, E):
             scalar_gather(e)
-        for e in range(1, E):
+        for e in range(G_EXPERTS, E):
             w_interleave(nc.vector.tensor_copy, e)
         for h in range(2):
             w_quantize(0, h)

@@ -1,6 +1,7 @@
 from contextlib import ExitStack
 
 import concourse.mybir as mybir
+from concourse.masks import make_identity
 
 K, T, E, C, N = 512, 1024, 8, 256, 256
 FLOPS = 2 * K * N * E * C
@@ -22,6 +23,7 @@ CHUNK = 512
 CHUNKS = E * C // CHUNK
 V_CHUNKS = 2
 HALF = E // 2
+T_SUM = 768
 G_EXPERTS = 3
 
 
@@ -121,7 +123,7 @@ def tile_routed_moe_kernel(tc, xT, w, gate, offs, pos1, pos2, out):
                 )
             nc.scalar.copy(y_sb[mb][:, c * CHUNK:(c + 1) * CHUNK], banks[(mb, c)][:])
 
-        def combine(mb, first, count):
+        def products(mb, first, count):
             prods = []
             for r in range(2):
                 prod = ring.tile([P, count], F32, name="prod%d_%d" % (r, count))
@@ -132,9 +134,29 @@ def tile_routed_moe_kernel(tc, xT, w, gate, offs, pos1, pos2, out):
                     MULT,
                 )
                 prods.append(prod)
+            return prods
+
+        def add_on_vector(mb, prods, skip, first, count):
             res = ring.tile([P, count], F32, name="res%d" % count)
-            nc.vector.tensor_tensor(res[:], prods[0][:], prods[1][:], ADD)
+            nc.vector.tensor_tensor(res[:], prods[0][:, skip:skip + count], prods[1][:, skip:skip + count], ADD)
             nc.sync.dma_start(out[mb * P:(mb + 1) * P, first:first + count], res[:])
+
+        def add_on_tensor(mb, prods, count):
+            res = keep.tile([P, count], F32, name="res_t")
+            for c in range(-(-count // CHUNK)):
+                width = min(CHUNK, count - c * CHUNK)
+                cols = slice(c * CHUNK, c * CHUNK + width)
+                acc = psum.tile([P, CHUNK], F32, name="bank%d_%d" % (mb, c))
+                for r in range(2):
+                    nc.tensor.matmul(acc[:, 0:width], lhsT=ident[:], rhs=prods[r][:, cols], start=(r == 0), stop=(r == 1))
+                nc.scalar.copy(res[:, cols], acc[:, 0:width])
+            nc.sync.dma_start(out[mb * P:(mb + 1) * P, 0:count], res[:])
+
+        def combine(mb, first, count):
+            add_on_vector(mb, products(mb, first, count), 0, first, count)
+
+        ident = keep.tile([P, P], F32, name="ident")
+        make_identity(nc, ident[:])
 
         warm = keep.tile([P, 2], F32, name="warm")
         nc.vector.memset(warm[:, 0:1], 0.0)
@@ -164,6 +186,8 @@ def tile_routed_moe_kernel(tc, xT, w, gate, offs, pos1, pos2, out):
             w_quantize(1, h)
         for c in range(CHUNKS):
             multiply(c, 1)
-        combine(0, 0, T)
+        first_block = products(0, 0, T)
+        add_on_tensor(0, first_block, T_SUM)
+        add_on_vector(0, first_block, T_SUM, T_SUM, T - T_SUM)
         combine(1, 0, 3 * T // 4)
         combine(1, 3 * T // 4, T // 4)

@@ -102,6 +102,12 @@ def tile_routed_moe_kernel(tc, xT, w, gate, offs, pos1, pos2, out):
         def w_interleave(copy, e):
             copy(w_grouped[:, :, e, :, :], w_raw[e][:].rearrange("p j (m n) -> p m n j", m=BLOCKS))
 
+        def w_interleave_by_fours(copy, e):
+            copy(
+                w_grouped[:, :, e, :, :].rearrange("p m (g i) j -> p m g j i", i=4),
+                w_raw[e][:].rearrange("p j (m g i) -> p m g j i", m=BLOCKS, i=4),
+            )
+
         def w_quantize(mb, h):
             cols = slice(h * HALF * P, (h + 1) * HALF * P)
             nc.vector.quantize_mx(
@@ -172,7 +178,7 @@ def tile_routed_moe_kernel(tc, xT, w, gate, offs, pos1, pos2, out):
         for e in range(2 * V_CHUNKS, E):
             scalar_gather(e)
         for e in range(G_EXPERTS, E):
-            w_interleave(nc.vector.tensor_copy, e)
+            w_interleave_by_fours(nc.vector.tensor_copy, e)
         for h in range(2):
             w_quantize(0, h)
         for c in range(V_CHUNKS):

@@ -42,7 +42,8 @@ def tile_routed_moe_kernel(tc, xT, w, gate, offs, pos1, pos2, out):
         w_raw.append(ring.tile([P, PACK, N], F32, name="turn", bufs=1, align_bytes=64))
         pos_t = [lists.tile([P, T // 16], U16, name="pos_t%d" % r) for r in range(2)]
         gate_t = {}
-        nc.sync.dma_start(x_plane[0][:], x_rows[:, 0, :])
+        for h in range(2):
+            nc.sync.dma_start(x_plane[0][:, h * (T // 2):(h + 1) * (T // 2)], x_rows[:, 0, h * (T // 2):(h + 1) * (T // 2)])
         nc.sync.dma_start(offs_t[:], offs)
         for t in range(1, PACK):
             nc.sync.dma_start(x_plane[t][:], x_rows[:, t, :])
@@ -70,7 +71,14 @@ def tile_routed_moe_kernel(tc, xT, w, gate, offs, pos1, pos2, out):
         x_grouped = {}
 
         def cast(t):
-            nc.vector.tensor_copy(x_bf[t][:], x_plane[t][:])
+            if t == 0:
+                for h in range(2):
+                    cols = slice(h * (T // 2), (h + 1) * (T // 2))
+                    nc.vector.tensor_copy(x_bf[t][:, cols], x_plane[t][:, cols])
+            elif t == 2:
+                nc.scalar.copy(x_bf[t][:], x_plane[t][:])
+            else:
+                nc.vector.tensor_copy(x_bf[t][:], x_plane[t][:])
 
         def gather(c):
             gathered[c] = ring.tile([P, PACK, CHUNK], F32, name="g4")
@@ -80,10 +88,20 @@ def tile_routed_moe_kernel(tc, xT, w, gate, offs, pos1, pos2, out):
 
         def x_interleave(c):
             x_grouped[c] = keep.tile([P, CHUNK, PACK], BF16, name="x_grp%d" % c, align_bytes=64)
-            nc.scalar.copy(
-                x_grouped[c][:].rearrange("p (g i) t -> p g t i", i=4),
-                gathered[c][:].rearrange("p t (g i) -> p g t i", i=4),
-            )
+            if c < V_CHUNKS - 1:
+                nc.scalar.copy(
+                    x_grouped[c][:].rearrange("p (g i) t -> p g t i", i=4),
+                    gathered[c][:].rearrange("p t (g i) -> p g t i", i=4),
+                )
+            else:
+                nc.scalar.copy(
+                    x_grouped[c][:, 0:C, :].rearrange("p (g i) t -> p g t i", i=4),
+                    gathered[c][:, :, 0:C].rearrange("p t (g i) -> p g t i", i=4),
+                )
+                nc.vector.tensor_copy(
+                    x_grouped[c][:, C:CHUNK, :].rearrange("p (g i) t -> p g t i", i=4),
+                    gathered[c][:, :, C:CHUNK].rearrange("p t (g i) -> p g t i", i=4),
+                )
 
         def scalar_gather(e):
             x_grouped[("s", e)] = keep.tile([P, C, PACK], BF16, name="x_grs%d" % e, align_bytes=64)

@@ -77,6 +77,8 @@ def tile_routed_moe_kernel(tc, xT, w, gate, offs, pos1, pos2, out):
                     nc.vector.tensor_copy(x_bf[t][:, cols], x_plane[t][:, cols])
             elif t == 2:
                 nc.scalar.copy(x_bf[t][:], x_plane[t][:])
+            elif t == 3:
+                nc.gpsimd.tensor_copy(x_bf[t][:], x_plane[t][:])
             else:
                 nc.vector.tensor_copy(x_bf[t][:], x_plane[t][:])
 

@@ -21,7 +21,8 @@ PACK = 4
 BLOCKS = N // P
 CHUNK = 512
 CHUNKS = E * C // CHUNK
-V_CHUNKS = 2
+V_EXPERTS = 3
+V_SLOTS = V_EXPERTS * C
 HALF = E // 2
 T_SUM = 768
 G_EXPERTS = 3
@@ -67,7 +68,8 @@ def tile_routed_moe_kernel(tc, xT, w, gate, offs, pos1, pos2, out):
         for mb in range(BLOCKS):
             for c in range(CHUNKS):
                 banks[(mb, c)] = psum.tile([P, CHUNK], F32, name="bank%d_%d" % (mb, c))
-        gathered = {}
+        gathered = keep.tile([P, PACK, V_SLOTS], F32, name="gathered")
+        x_grouped_v = keep.tile([P, V_SLOTS, PACK], BF16, name="x_grouped_v", align_bytes=64)
         x_grouped = {}
 
         def cast(t):
@@ -75,35 +77,21 @@ def tile_routed_moe_kernel(tc, xT, w, gate, offs, pos1, pos2, out):
                 for h in range(2):
                     cols = slice(h * (T // 2), (h + 1) * (T // 2))
                     nc.vector.tensor_copy(x_bf[t][:, cols], x_plane[t][:, cols])
-            elif t == 2:
-                nc.scalar.copy(x_bf[t][:], x_plane[t][:])
             elif t == 3:
                 nc.gpsimd.tensor_copy(x_bf[t][:], x_plane[t][:])
             else:
                 nc.vector.tensor_copy(x_bf[t][:], x_plane[t][:])
 
-        def gather(c):
-            gathered[c] = ring.tile([P, PACK, CHUNK], F32, name="g4")
-            slot_list = offs_t[:, c * (CHUNK // 16):(c + 1) * (CHUNK // 16)]
+        def gather():
+            slot_list = offs_t[:, 0:V_SLOTS // 16]
             for t in range(PACK):
-                nc.vector.tensor_copy(gathered[c][:, t, :], x_plane[t][:].indirect(slot_list))
+                nc.vector.tensor_copy(gathered[:, t, :], x_plane[t][:].indirect(slot_list))
 
-        def x_interleave(c):
-            x_grouped[c] = keep.tile([P, CHUNK, PACK], BF16, name="x_grp%d" % c, align_bytes=64)
-            if c < V_CHUNKS - 1:
-                nc.scalar.copy(
-                    x_grouped[c][:].rearrange("p (g i) t -> p g t i", i=4),
-                    gathered[c][:].rearrange("p t (g i) -> p g t i", i=4),
-                )
-            else:
-                nc.scalar.copy(
-                    x_grouped[c][:, 0:C, :].rearrange("p (g i) t -> p g t i", i=4),
-                    gathered[c][:, :, 0:C].rearrange("p t (g i) -> p g t i", i=4),
-                )
-                nc.vector.tensor_copy(
-                    x_grouped[c][:, C:CHUNK, :].rearrange("p (g i) t -> p g t i", i=4),
-                    gathered[c][:, :, C:CHUNK].rearrange("p t (g i) -> p g t i", i=4),
-                )
+        def x_interleave():
+            nc.vector.tensor_copy(
+                x_grouped_v[:].rearrange("p (g i) t -> p g t i", i=4),
+                gathered[:].rearrange("p t (g i) -> p g t i", i=4),
+            )
 
         def scalar_gather(e):
             x_grouped[("s", e)] = keep.tile([P, C, PACK], BF16, name="x_grs%d" % e, align_bytes=64)
@@ -111,12 +99,16 @@ def tile_routed_moe_kernel(tc, xT, w, gate, offs, pos1, pos2, out):
             for t in range(PACK):
                 nc.scalar.activation(x_grouped[("s", e)][:, :, t], x_bf[t][:].indirect(slot_list), COPY)
 
-        def x_quantize(key, first, count):
+        def x_quantize(first, count):
             cols = slice(first, first + count)
+            if first < V_SLOTS:
+                values = x_grouped_v[:, cols, :]
+            else:
+                values = x_grouped[("s", first // C)][:]
             nc.vector.quantize_mx(
                 out=x_codes[:, cols].bitcast(FP8X4),
                 scales=x_scales[:, cols],
-                in_=x_grouped[key][:].rearrange("p n t -> p (n t)"),
+                in_=values.rearrange("p n t -> p (n t)"),
             )
 
         def w_interleave(copy, e):
@@ -192,21 +184,19 @@ def tile_routed_moe_kernel(tc, xT, w, gate, offs, pos1, pos2, out):
             cast(t)
         for e in range(G_EXPERTS):
             w_interleave(nc.gpsimd.tensor_copy, e)
-        for c in range(V_CHUNKS):
-            gather(c)
-            x_interleave(c)
-        for e in range(2 * V_CHUNKS, E):
+        gather()
+        x_interleave()
+        for e in range(V_EXPERTS, E):
             scalar_gather(e)
         for e in range(G_EXPERTS, E):
             w_interleave_by_fours(nc.vector.tensor_copy, e)
         for h in range(2):
             w_quantize(0, h)
-        for c in range(V_CHUNKS):
-            x_quantize(c, c * CHUNK, CHUNK)
-            multiply(c, 0)
-        for c in range(V_CHUNKS, CHUNKS):
+        x_quantize(0, CHUNK)
+        multiply(0, 0)
+        for c in range(1, CHUNKS):
             for e in (2 * c, 2 * c + 1):
-                x_quantize(("s", e), e * C, C)
+                x_quantize(e * C, C)
             multiply(c, 0)
         for h in range(2):
             w_quantize(1, h)

@@ -25,7 +25,7 @@ V_EXPERTS = 3
 V_SLOTS = V_EXPERTS * C
 HALF = E // 2
 T_SUM = 768
-G_EXPERTS = 3
+G_EXPERTS = 2
 
 
 def tile_routed_moe_kernel(tc, xT, w, gate, offs, pos1, pos2, out):

@@ -25,7 +25,7 @@ V_EXPERTS = 3
 V_SLOTS = V_EXPERTS * C
 HALF = E // 2
 T_SUM = 768
-G_EXPERTS = 2
+G_EXPERTS = 1
 
 
 def tile_routed_moe_kernel(tc, xT, w, gate, offs, pos1, pos2, out):
@@ -77,10 +77,8 @@ def tile_routed_moe_kernel(tc, xT, w, gate, offs, pos1, pos2, out):
                 for h in range(2):
                     cols = slice(h * (T // 2), (h + 1) * (T // 2))
                     nc.vector.tensor_copy(x_bf[t][:, cols], x_plane[t][:, cols])
-            elif t == 3:
-                nc.gpsimd.tensor_copy(x_bf[t][:], x_plane[t][:])
             else:
-                nc.vector.tensor_copy(x_bf[t][:], x_plane[t][:])
+                nc.gpsimd.tensor_copy(x_bf[t][:], x_plane[t][:])
 
         def gather():
             slot_list = offs_t[:, 0:V_SLOTS // 16]

@@ -21,8 +21,9 @@ PACK = 4
 BLOCKS = N // P
 CHUNK = 512
 CHUNKS = E * C // CHUNK
-V_EXPERTS = 3
-V_SLOTS = V_EXPERTS * C
+V_SLOTS = 768
+V_PIECES = [(first, min(CHUNK, V_SLOTS - first)) for first in range(0, V_SLOTS, CHUNK)]
+S_PIECES = [(first, min(C - first % C, E * C - first)) for first in [V_SLOTS] + list(range((V_SLOTS // C + 1) * C, E * C, C))]
 HALF = E // 2
 T_SUM = 768
 G_EXPERTS = 1
@@ -71,6 +72,7 @@ def tile_routed_moe_kernel(tc, xT, w, gate, offs, pos1, pos2, out):
         gathered = keep.tile([P, PACK, V_SLOTS], F32, name="gathered")
         x_grouped_v = keep.tile([P, V_SLOTS, PACK], BF16, name="x_grouped_v", align_bytes=64)
         x_grouped = {}
+        x_pairs = {}
 
         def cast(t):
             if t == 0:
@@ -91,18 +93,25 @@ def tile_routed_moe_kernel(tc, xT, w, gate, offs, pos1, pos2, out):
                 gathered[:].rearrange("p t (g i) -> p g t i", i=4),
             )
 
-        def scalar_gather(e):
-            x_grouped[("s", e)] = keep.tile([P, C, PACK], BF16, name="x_grs%d" % e, align_bytes=64)
-            slot_list = offs_t[:, e * (C // 16):(e + 1) * (C // 16)]
+        def scalar_gather(first, count):
+            x_pairs[first] = keep.tile([P, 2, count, 2], BF16, name="x_pairs%d" % first, align_bytes=64)
+            slot_list = offs_t[:, first // 16:(first + count) // 16]
             for t in range(PACK):
-                nc.scalar.activation(x_grouped[("s", e)][:, :, t], x_bf[t][:].indirect(slot_list), COPY)
+                nc.scalar.activation(x_pairs[first][:, t // 2, :, t % 2], x_bf[t][:].indirect(slot_list), COPY)
+
+        def merge_pairs(first, count):
+            x_grouped[first] = keep.tile([P, count, PACK], BF16, name="x_grs%d" % first, align_bytes=64)
+            nc.scalar.copy(
+                x_grouped[first][:].rearrange("p n t -> p (n t)").bitcast(F32).rearrange("p (n u) -> p n u", u=2),
+                x_pairs[first][:].rearrange("p u n i -> p (u n i)").bitcast(F32).rearrange("p (u n) -> p n u", u=2),
+            )
 
         def x_quantize(first, count):
             cols = slice(first, first + count)
             if first < V_SLOTS:
                 values = x_grouped_v[:, cols, :]
             else:
-                values = x_grouped[("s", first // C)][:]
+                values = x_grouped[first][:]
             nc.vector.quantize_mx(
                 out=x_codes[:, cols].bitcast(FP8X4),
                 scales=x_scales[:, cols],
@@ -184,17 +193,18 @@ def tile_routed_moe_kernel(tc, xT, w, gate, offs, pos1, pos2, out):
             w_interleave(nc.gpsimd.tensor_copy, e)
         gather()
         x_interleave()
-        for e in range(V_EXPERTS, E):
-            scalar_gather(e)
+        for first, count in S_PIECES:
+            scalar_gather(first, count)
+        for first, count in S_PIECES:
+            merge_pairs(first, count)
         for e in range(G_EXPERTS, E):
             w_interleave_by_fours(nc.vector.tensor_copy, e)
         for h in range(2):
             w_quantize(0, h)
-        x_quantize(0, CHUNK)
-        multiply(0, 0)
-        for c in range(1, CHUNKS):
-            for e in (2 * c, 2 * c + 1):
-                x_quantize(e * C, C)
+        for c in range(CHUNKS):
+            for first, count in V_PIECES + S_PIECES:
+                if first // CHUNK == c:
+                    x_quantize(first, count)
             multiply(c, 0)
         for h in range(2):
             w_quantize(1, h)

@@ -27,6 +27,7 @@ S_PIECES = [(first, min(C - first % C, E * C - first)) for first in [V_SLOTS] + 
 HALF = E // 2
 T_SUM = 768
 G_EXPERTS = 1
+V_MERGES = 1
 
 
 def tile_routed_moe_kernel(tc, xT, w, gate, offs, pos1, pos2, out):
@@ -101,7 +102,8 @@ def tile_routed_moe_kernel(tc, xT, w, gate, offs, pos1, pos2, out):
 
         def merge_pairs(first, count):
             x_grouped[first] = keep.tile([P, count, PACK], BF16, name="x_grs%d" % first, align_bytes=64)
-            nc.scalar.copy(
+            copy = nc.vector.tensor_copy if (first, count) in S_PIECES[:V_MERGES] else nc.scalar.copy
+            copy(
                 x_grouped[first][:].rearrange("p n t -> p (n t)").bitcast(F32).rearrange("p (n u) -> p n u", u=2),
                 x_pairs[first][:].rearrange("p u n i -> p (u n i)").bitcast(F32).rearrange("p (u n) -> p n u", u=2),
             )

@@ -28,6 +28,7 @@ HALF = E // 2
 T_SUM = 768
 G_EXPERTS = 1
 V_MERGES = 1
+S_HALVES = 2
 
 
 def tile_routed_moe_kernel(tc, xT, w, gate, offs, pos1, pos2, out):
@@ -129,6 +130,12 @@ def tile_routed_moe_kernel(tc, xT, w, gate, offs, pos1, pos2, out):
                 w_raw[e][:].rearrange("p j (m g i) -> p m g j i", m=BLOCKS, i=4),
             )
 
+        def w_interleave_half(copy, e, mb):
+            copy(
+                w_grouped[:, mb, e, :, :].rearrange("p (g i) j -> p g j i", i=4),
+                w_raw[e][:, :, mb * P:(mb + 1) * P].rearrange("p j (g i) -> p g j i", i=4),
+            )
+
         def w_quantize(mb, h):
             cols = slice(h * HALF * P, (h + 1) * HALF * P)
             nc.vector.quantize_mx(
@@ -199,7 +206,10 @@ def tile_routed_moe_kernel(tc, xT, w, gate, offs, pos1, pos2, out):
             scalar_gather(first, count)
         for first, count in S_PIECES:
             merge_pairs(first, count)
-        for e in range(G_EXPERTS, E):
+        for e in range(G_EXPERTS, G_EXPERTS + S_HALVES):
+            w_interleave_half(nc.vector.tensor_copy, e, 0)
+            w_interleave_half(nc.scalar.copy, e, 1)
+        for e in range(G_EXPERTS + S_HALVES, E):
             w_interleave_by_fours(nc.vector.tensor_copy, e)
         for h in range(2):
             w_quantize(0, h)

@@ -28,7 +28,7 @@ HALF = E // 2
 T_SUM = 768
 G_EXPERTS = 1
 V_MERGES = 1
-S_HALVES = 2
+S_HALVES = 1
 
 
 def tile_routed_moe_kernel(tc, xT, w, gate, offs, pos1, pos2, out):

@@ -22,7 +22,7 @@ BLOCKS = N // P
 CHUNK = 512
 CHUNKS = E * C // CHUNK
 V_SLOTS = 768
-V_PIECES = [(first, min(CHUNK, V_SLOTS - first)) for first in range(0, V_SLOTS, CHUNK)]
+V_PIECES = [(first, C) for first in range(0, V_SLOTS, C)]
 S_PIECES = [(first, min(C - first % C, E * C - first)) for first in [V_SLOTS] + list(range((V_SLOTS // C + 1) * C, E * C, C))]
 HALF = E // 2
 T_SUM = 768
@@ -71,8 +71,6 @@ def tile_routed_moe_kernel(tc, xT, w, gate, offs, pos1, pos2, out):
         for mb in range(BLOCKS):
             for c in range(CHUNKS):
                 banks[(mb, c)] = psum.tile([P, CHUNK], F32, name="bank%d_%d" % (mb, c))
-        gathered = keep.tile([P, PACK, V_SLOTS], F32, name="gathered")
-        x_grouped_v = keep.tile([P, V_SLOTS, PACK], BF16, name="x_grouped_v", align_bytes=64)
         x_grouped = {}
         x_pairs = {}
 
@@ -85,15 +83,12 @@ def tile_routed_moe_kernel(tc, xT, w, gate, offs, pos1, pos2, out):
                 nc.gpsimd.tensor_copy(x_bf[t][:], x_plane[t][:])
 
         def gather():
-            slot_list = offs_t[:, 0:V_SLOTS // 16]
+            for first, count in V_PIECES:
+                x_pairs[first] = keep.tile([P, 2, count, 2], BF16, name="x_pairs%d" % first, align_bytes=64)
             for t in range(PACK):
-                nc.vector.tensor_copy(gathered[:, t, :], x_plane[t][:].indirect(slot_list))
-
-        def x_interleave():
-            nc.vector.tensor_copy(
-                x_grouped_v[:].rearrange("p (g i) t -> p g t i", i=4),
-                gathered[:].rearrange("p t (g i) -> p g t i", i=4),
-            )
+                for first, count in V_PIECES:
+                    slot_list = offs_t[:, first // 16:(first + count) // 16]
+                    nc.vector.tensor_copy(x_pairs[first][:, t // 2, :, t % 2], x_plane[t][:].indirect(slot_list))
 
         def scalar_gather(first, count):
             x_pairs[first] = keep.tile([P, 2, count, 2], BF16, name="x_pairs%d" % first, align_bytes=64)
@@ -103,7 +98,7 @@ def tile_routed_moe_kernel(tc, xT, w, gate, offs, pos1, pos2, out):
 
         def merge_pairs(first, count):
             x_grouped[first] = keep.tile([P, count, PACK], BF16, name="x_grs%d" % first, align_bytes=64)
-            copy = nc.vector.tensor_copy if (first, count) in S_PIECES[:V_MERGES] else nc.scalar.copy
+            copy = nc.vector.tensor_copy if (first, count) in V_PIECES + S_PIECES[:V_MERGES] else nc.scalar.copy
             copy(
                 x_grouped[first][:].rearrange("p n t -> p (n t)").bitcast(F32).rearrange("p (n u) -> p n u", u=2),
                 x_pairs[first][:].rearrange("p u n i -> p (u n i)").bitcast(F32).rearrange("p (u n) -> p n u", u=2),
@@ -111,10 +106,7 @@ def tile_routed_moe_kernel(tc, xT, w, gate, offs, pos1, pos2, out):
 
         def x_quantize(first, count):
             cols = slice(first, first + count)
-            if first < V_SLOTS:
-                values = x_grouped_v[:, cols, :]
-            else:
-                values = x_grouped[first][:]
+            values = x_grouped[first][:]
             nc.vector.quantize_mx(
                 out=x_codes[:, cols].bitcast(FP8X4),
                 scales=x_scales[:, cols],
@@ -201,7 +193,8 @@ def tile_routed_moe_kernel(tc, xT, w, gate, offs, pos1, pos2, out):
         for e in range(G_EXPERTS):
             w_interleave(nc.gpsimd.tensor_copy, e)
         gather()
-        x_interleave()
+        for first, count in V_PIECES:
+            merge_pairs(first, count)
         for first, count in S_PIECES:
             scalar_gather(first, count)
         for first, count in S_PIECES:

@@ -192,6 +192,7 @@ def tile_routed_moe_kernel(tc, xT, w, gate, offs, pos1, pos2, out):
             cast(t)
         for e in range(G_EXPERTS):
             w_interleave(nc.gpsimd.tensor_copy, e)
+        nc.gpsimd.tensor_copy(w_grouped[:, 1, G_EXPERTS, :, :], w_raw[G_EXPERTS][:, :, P:2 * P].rearrange("p j n -> p n j"))
         gather()
         for first, count in V_PIECES:
             merge_pairs(first, count)
@@ -199,10 +200,11 @@ def tile_routed_moe_kernel(tc, xT, w, gate, offs, pos1, pos2, out):
             scalar_gather(first, count)
         for first, count in S_PIECES:
             merge_pairs(first, count)
-        for e in range(G_EXPERTS, G_EXPERTS + S_HALVES):
+        w_interleave_half(nc.vector.tensor_copy, G_EXPERTS, 0)
+        for e in range(G_EXPERTS + 1, G_EXPERTS + 1 + S_HALVES):
             w_interleave_half(nc.vector.tensor_copy, e, 0)
             w_interleave_half(nc.scalar.copy, e, 1)
-        for e in range(G_EXPERTS + S_HALVES, E):
+        for e in range(G_EXPERTS + 1 + S_HALVES, E):
             w_interleave_by_fours(nc.vector.tensor_copy, e)
         for h in range(2):
             w_quantize(0, h)

@@ -62,7 +62,7 @@ def tile_routed_moe_kernel(tc, xT, w, gate, offs, pos1, pos2, out):
 
         x_bf = [keep.tile([P, T], BF16, name="x_bf%d" % t) for t in range(PACK)]
         x_codes = keep.tile([P, E * C], U32, name="x_codes", align_bytes=64)
-        x_scales = ring.tile([P, E * C], U8, name="turn", bufs=1, align_bytes=64)
+        x_scales = [keep.tile([P, HALF * C], U8, name="x_scales0", align_bytes=64), ring.tile([P, HALF * C], U8, name="turn", bufs=1, align_bytes=64)]
         w_grouped = keep.tile([P, BLOCKS, E, P, PACK], BF16, name="w_grouped", align_bytes=64)
         w_codes = [keep.tile([P, E * P], U32, name="w_codes%d" % mb, align_bytes=64) for mb in range(BLOCKS)]
         w_scales = [keep.tile([P, E * P], U8, name="w_scales%d" % mb, align_bytes=64) for mb in range(BLOCKS)]
@@ -109,7 +109,7 @@ def tile_routed_moe_kernel(tc, xT, w, gate, offs, pos1, pos2, out):
             values = x_grouped[first][:]
             nc.vector.quantize_mx(
                 out=x_codes[:, cols].bitcast(FP8X4),
-                scales=x_scales[:, cols],
+                scales=x_scales[first // (HALF * C)][:, first % (HALF * C):first % (HALF * C) + count],
                 in_=values.rearrange("p n t -> p (n t)"),
             )
 
@@ -143,7 +143,7 @@ def tile_routed_moe_kernel(tc, xT, w, gate, offs, pos1, pos2, out):
                     lhsT=w_codes[mb][:, e * P:(e + 1) * P].bitcast(FP8X4),
                     lhsT_scale=w_scales[mb][:, e * P:(e + 1) * P],
                     rhs=x_codes[:, e * C:(e + 1) * C].bitcast(FP8X4),
-                    rhs_scale=x_scales[:, e * C:(e + 1) * C],
+                    rhs_scale=x_scales[e // HALF][:, (e % HALF) * C:(e % HALF + 1) * C],
                     start=True,
                     stop=True,
                 )

@@ -28,7 +28,7 @@ HALF = E // 2
 T_SUM = 768
 G_EXPERTS = 1
 V_MERGES = 1
-S_HALVES = 1
+S_HALVES = 0
 
 
 def tile_routed_moe_kernel(tc, xT, w, gate, offs, pos1, pos2, out):
@@ -74,6 +74,11 @@ def tile_routed_moe_kernel(tc, xT, w, gate, offs, pos1, pos2, out):
         x_grouped = {}
         x_pairs = {}
 
+        def quantize_pieces(first, count):
+            if first + count == E * C:
+                return [(first, count // 2), (first + count // 2, count // 2)]
+            return [(first, count)]
+
         def cast(t):
             if t == 0:
                 for h in range(2):
@@ -97,12 +102,13 @@ def tile_routed_moe_kernel(tc, xT, w, gate, offs, pos1, pos2, out):
                 nc.scalar.activation(x_pairs[first][:, t // 2, :, t % 2], x_bf[t][:].indirect(slot_list), COPY)
 
         def merge_pairs(first, count):
-            x_grouped[first] = keep.tile([P, count, PACK], BF16, name="x_grs%d" % first, align_bytes=64)
             copy = nc.vector.tensor_copy if (first, count) in V_PIECES + S_PIECES[:V_MERGES] else nc.scalar.copy
-            copy(
-                x_grouped[first][:].rearrange("p n t -> p (n t)").bitcast(F32).rearrange("p (n u) -> p n u", u=2),
-                x_pairs[first][:].rearrange("p u n i -> p (u n i)").bitcast(F32).rearrange("p (u n) -> p n u", u=2),
-            )
+            for start, width in quantize_pieces(first, count):
+                x_grouped[start] = keep.tile([P, width, PACK], BF16, name="x_grs%d" % start, align_bytes=64)
+                copy(
+                    x_grouped[start][:].rearrange("p n t -> p (n t)").bitcast(F32).rearrange("p (n u) -> p n u", u=2),
+                    x_pairs[first][:].rearrange("p u n i -> p (u n i)").bitcast(F32).rearrange("p (u n) -> p n u", u=2)[:, start - first:start - first + width, :],
+                )
 
         def x_quantize(first, count):
             cols = slice(first, first + count)
@@ -136,18 +142,26 @@ def tile_routed_moe_kernel(tc, xT, w, gate, offs, pos1, pos2, out):
                 in_=w_grouped[:, mb, h * HALF:(h + 1) * HALF, :, :].rearrange("p e n j -> p (e n j)"),
             )
 
+        def multiply_slots(mb, first, count):
+            e = first // C
+            nc.tensor.matmul_mx(
+                out=banks[(mb, first // CHUNK)][:, first % CHUNK:first % CHUNK + count],
+                lhsT=w_codes[mb][:, e * P:(e + 1) * P].bitcast(FP8X4),
+                lhsT_scale=w_scales[mb][:, e * P:(e + 1) * P],
+                rhs=x_codes[:, first:first + count].bitcast(FP8X4),
+                rhs_scale=x_scales[e // HALF][:, first % (HALF * C):first % (HALF * C) + count],
+                start=True,
+                stop=True,
+            )
+
+        def leave_bank(mb, first, count):
+            nc.scalar.copy(y_sb[mb][:, first:first + count], banks[(mb, first // CHUNK)][:, first % CHUNK:first % CHUNK + count])
+
         def multiply(c, mb):
             for e in (2 * c, 2 * c + 1):
-                nc.tensor.matmul_mx(
-                    out=banks[(mb, c)][:, (e % 2) * C:(e % 2 + 1) * C],
-                    lhsT=w_codes[mb][:, e * P:(e + 1) * P].bitcast(FP8X4),
-                    lhsT_scale=w_scales[mb][:, e * P:(e + 1) * P],
-                    rhs=x_codes[:, e * C:(e + 1) * C].bitcast(FP8X4),
-                    rhs_scale=x_scales[e // HALF][:, (e % HALF) * C:(e % HALF + 1) * C],
-                    start=True,
-                    stop=True,
-                )
-            nc.scalar.copy(y_sb[mb][:, c * CHUNK:(c + 1) * CHUNK], banks[(mb, c)][:])
+                for first, count in quantize_pieces(e * C, C):
+                    multiply_slots(mb, first, count)
+            leave_bank(mb, c * CHUNK, CHUNK)
 
         def products(mb, first, count):
             prods = []
@@ -208,11 +222,16 @@ def tile_routed_moe_kernel(tc, xT, w, gate, offs, pos1, pos2, out):
             w_interleave_by_fours(nc.vector.tensor_copy, e)
         for h in range(2):
             w_quantize(0, h)
-        for c in range(CHUNKS):
+        for c in range(CHUNKS - 1):
             for first, count in V_PIECES + S_PIECES:
                 if first // CHUNK == c:
                     x_quantize(first, count)
             multiply(c, 0)
+        for e in (E - 2, E - 1):
+            for first, count in quantize_pieces(e * C, C):
+                x_quantize(first, count)
+                multiply_slots(0, first, count)
+        leave_bank(0, (CHUNKS - 1) * CHUNK, CHUNK)
         for h in range(2):
             w_quantize(1, h)
         for c in range(CHUNKS):

@@ -70,7 +70,8 @@ def tile_routed_moe_kernel(tc, xT, w, gate, offs, pos1, pos2, out):
         banks = {}
         for mb in range(BLOCKS):
             for c in range(CHUNKS):
-                banks[(mb, c)] = psum.tile([P, CHUNK], F32, name="bank%d_%d" % (mb, c))
+                banks[(mb, c)] = psum.tile([P, CHUNK], F32, name="bank0_0" if (mb, c) == (1, 0) else "bank%d_%d" % (mb, c))
+        last_bank = psum.tile([P, CHUNK], F32, name="bank1_0")
         x_grouped = {}
         x_pairs = {}
 
@@ -142,10 +143,15 @@ def tile_routed_moe_kernel(tc, xT, w, gate, offs, pos1, pos2, out):
                 in_=w_grouped[:, mb, h * HALF:(h + 1) * HALF, :, :].rearrange("p e n j -> p (e n j)"),
             )
 
+        def bank_columns(mb, first, count):
+            if mb == 0 and first // C == E - 1:
+                return last_bank[:, first % C:first % C + count]
+            return banks[(mb, first // CHUNK)][:, first % CHUNK:first % CHUNK + count]
+
         def multiply_slots(mb, first, count):
             e = first // C
             nc.tensor.matmul_mx(
-                out=banks[(mb, first // CHUNK)][:, first % CHUNK:first % CHUNK + count],
+                out=bank_columns(mb, first, count),
                 lhsT=w_codes[mb][:, e * P:(e + 1) * P].bitcast(FP8X4),
                 lhsT_scale=w_scales[mb][:, e * P:(e + 1) * P],
                 rhs=x_codes[:, first:first + count].bitcast(FP8X4),
@@ -155,7 +161,7 @@ def tile_routed_moe_kernel(tc, xT, w, gate, offs, pos1, pos2, out):
             )
 
         def leave_bank(mb, first, count):
-            nc.scalar.copy(y_sb[mb][:, first:first + count], banks[(mb, first // CHUNK)][:, first % CHUNK:first % CHUNK + count])
+            nc.scalar.copy(y_sb[mb][:, first:first + count], bank_columns(mb, first, count))
 
         def multiply(c, mb):
             for e in (2 * c, 2 * c + 1):
@@ -231,7 +237,7 @@ def tile_routed_moe_kernel(tc, xT, w, gate, offs, pos1, pos2, out):
             for first, count in quantize_pieces(e * C, C):
                 x_quantize(first, count)
                 multiply_slots(0, first, count)
-        leave_bank(0, (CHUNKS - 1) * CHUNK, CHUNK)
+            leave_bank(0, e * C, C)
         for h in range(2):
             w_quantize(1, h)
         for c in range(CHUNKS):

from contextlib import ExitStack

import concourse.mybir as mybir
from concourse.masks import make_identity

K, T, E, C, N = 512, 1024, 8, 256, 256
FLOPS = 2 * K * N * E * C

F32 = mybir.dt.float32
BF16 = mybir.dt.bfloat16
U32 = mybir.dt.uint32
U16 = mybir.dt.uint16
U8 = mybir.dt.uint8
FP8X4 = mybir.dt.float8_e4m3fn_x4
MULT = mybir.AluOpType.mult
ADD = mybir.AluOpType.add
COPY = mybir.ActivationFunctionType.Copy

P = 128
PACK = 4
BLOCKS = N // P
CHUNK = 512
CHUNKS = E * C // CHUNK
V_SLOTS = 768
V_PIECES = [(first, C) for first in range(0, V_SLOTS, C)]
S_PIECES = [(first, min(C - first % C, E * C - first)) for first in [V_SLOTS] + list(range((V_SLOTS // C + 1) * C, E * C, C))]
HALF = E // 2
T_SUM = 768
G_EXPERTS = 1
V_MERGES = 1
S_HALVES = 0


def tile_routed_moe_kernel(tc, xT, w, gate, offs, pos1, pos2, out):
    nc = tc.nc
    with ExitStack() as ctx:
        lists = ctx.enter_context(tc.tile_pool(name="lists", bufs=1))
        keep = ctx.enter_context(tc.tile_pool(name="keep", bufs=1))
        ring = ctx.enter_context(tc.tile_pool(name="ring", bufs=2))
        psum = ctx.enter_context(tc.psum_pool(name="psum", bufs=1))

        offs_t = lists.tile([P, E * C // 16], U16, name="offs_t")
        x_rows = xT.rearrange("(p t) n -> p t n", t=PACK)
        x_plane = [keep.tile([P, T], F32, name="x_plane%d" % t) for t in range(PACK)]
        w_raw = [keep.tile([P, PACK, N], F32, name="w_raw%d" % e) for e in range(E - 1)]
        w_raw.append(ring.tile([P, PACK, N], F32, name="turn", bufs=1, align_bytes=64))
        pos_t = [lists.tile([P, T // 16], U16, name="pos_t%d" % r) for r in range(2)]
        gate_t = {}
        for h in range(2):
            nc.sync.dma_start(x_plane[0][:, h * (T // 2):(h + 1) * (T // 2)], x_rows[:, 0, h * (T // 2):(h + 1) * (T // 2)])
        nc.sync.dma_start(offs_t[:], offs)
        for t in range(1, PACK):
            nc.sync.dma_start(x_plane[t][:], x_rows[:, t, :])
        for e in range(E):
            nc.sync.dma_start(w_raw[e][:], w[e].rearrange("(p j) n -> p j n", j=PACK))
        for r in range(2):
            nc.sync.dma_start(pos_t[r][:], (pos1, pos2)[r])
        for mb in range(BLOCKS):
            for r in range(2):
                gate_t[(r, mb)] = keep.tile([P, T], F32, name="gate_t%d_%d" % (r, mb))
                nc.sync.dma_start(gate_t[(r, mb)][:], gate[r, mb * P:(mb + 1) * P, :])

        x_bf = [keep.tile([P, T], BF16, name="x_bf%d" % t) for t in range(PACK)]
        x_codes = keep.tile([P, E * C], U32, name="x_codes", align_bytes=64)
        x_scales = [keep.tile([P, HALF * C], U8, name="x_scales0", align_bytes=64), ring.tile([P, HALF * C], U8, name="turn", bufs=1, align_bytes=64)]
        w_grouped = keep.tile([P, BLOCKS, E, P, PACK], BF16, name="w_grouped", align_bytes=64)
        w_codes = [keep.tile([P, E * P], U32, name="w_codes%d" % mb, align_bytes=64) for mb in range(BLOCKS)]
        w_scales = [keep.tile([P, E * P], U8, name="w_scales%d" % mb, align_bytes=64) for mb in range(BLOCKS)]
        y_sb = [keep.tile([P, E * C], F32, name="y_sb%d" % mb) for mb in range(BLOCKS)]
        banks = {}
        for mb in range(BLOCKS):
            for c in range(CHUNKS):
                banks[(mb, c)] = psum.tile([P, CHUNK], F32, name="bank0_0" if (mb, c) == (1, 0) else "bank%d_%d" % (mb, c))
        last_bank = psum.tile([P, CHUNK], F32, name="bank1_0")
        x_grouped = {}
        x_pairs = {}

        def quantize_pieces(first, count):
            if first + count == E * C:
                return [(first, count // 2), (first + count // 2, count // 2)]
            return [(first, count)]

        def cast(t):
            if t == 0:
                for h in range(2):
                    cols = slice(h * (T // 2), (h + 1) * (T // 2))
                    nc.vector.tensor_copy(x_bf[t][:, cols], x_plane[t][:, cols])
            else:
                nc.gpsimd.tensor_copy(x_bf[t][:], x_plane[t][:])

        def gather():
            for first, count in V_PIECES:
                x_pairs[first] = keep.tile([P, 2, count, 2], BF16, name="x_pairs%d" % first, align_bytes=64)
            for t in range(PACK):
                for first, count in V_PIECES:
                    slot_list = offs_t[:, first // 16:(first + count) // 16]
                    nc.vector.tensor_copy(x_pairs[first][:, t // 2, :, t % 2], x_plane[t][:].indirect(slot_list))

        def scalar_gather(first, count):
            x_pairs[first] = keep.tile([P, 2, count, 2], BF16, name="x_pairs%d" % first, align_bytes=64)
            slot_list = offs_t[:, first // 16:(first + count) // 16]
            for t in range(PACK):
                nc.scalar.activation(x_pairs[first][:, t // 2, :, t % 2], x_bf[t][:].indirect(slot_list), COPY)

        def merge_pairs(first, count):
            copy = nc.vector.tensor_copy if (first, count) in V_PIECES + S_PIECES[:V_MERGES] else nc.scalar.copy
            for start, width in quantize_pieces(first, count):
                x_grouped[start] = keep.tile([P, width, PACK], BF16, name="x_grs%d" % start, align_bytes=64)
                copy(
                    x_grouped[start][:].rearrange("p n t -> p (n t)").bitcast(F32).rearrange("p (n u) -> p n u", u=2),
                    x_pairs[first][:].rearrange("p u n i -> p (u n i)").bitcast(F32).rearrange("p (u n) -> p n u", u=2)[:, start - first:start - first + width, :],
                )

        def x_quantize(first, count):
            cols = slice(first, first + count)
            values = x_grouped[first][:]
            nc.vector.quantize_mx(
                out=x_codes[:, cols].bitcast(FP8X4),
                scales=x_scales[first // (HALF * C)][:, first % (HALF * C):first % (HALF * C) + count],
                in_=values.rearrange("p n t -> p (n t)"),
            )

        def w_interleave(copy, e):
            copy(w_grouped[:, :, e, :, :], w_raw[e][:].rearrange("p j (m n) -> p m n j", m=BLOCKS))

        def w_interleave_by_fours(copy, e):
            copy(
                w_grouped[:, :, e, :, :].rearrange("p m (g i) j -> p m g j i", i=4),
                w_raw[e][:].rearrange("p j (m g i) -> p m g j i", m=BLOCKS, i=4),
            )

        def w_interleave_half(copy, e, mb):
            copy(
                w_grouped[:, mb, e, :, :].rearrange("p (g i) j -> p g j i", i=4),
                w_raw[e][:, :, mb * P:(mb + 1) * P].rearrange("p j (g i) -> p g j i", i=4),
            )

        def w_quantize(mb, h):
            cols = slice(h * HALF * P, (h + 1) * HALF * P)
            nc.vector.quantize_mx(
                out=w_codes[mb][:, cols].bitcast(FP8X4),
                scales=w_scales[mb][:, cols],
                in_=w_grouped[:, mb, h * HALF:(h + 1) * HALF, :, :].rearrange("p e n j -> p (e n j)"),
            )

        def bank_columns(mb, first, count):
            if mb == 0 and first // C == E - 1:
                return last_bank[:, first % C:first % C + count]
            return banks[(mb, first // CHUNK)][:, first % CHUNK:first % CHUNK + count]

        def multiply_slots(mb, first, count):
            e = first // C
            nc.tensor.matmul_mx(
                out=bank_columns(mb, first, count),
                lhsT=w_codes[mb][:, e * P:(e + 1) * P].bitcast(FP8X4),
                lhsT_scale=w_scales[mb][:, e * P:(e + 1) * P],
                rhs=x_codes[:, first:first + count].bitcast(FP8X4),
                rhs_scale=x_scales[e // HALF][:, first % (HALF * C):first % (HALF * C) + count],
                start=True,
                stop=True,
            )

        def leave_bank(mb, first, count):
            nc.scalar.copy(y_sb[mb][:, first:first + count], bank_columns(mb, first, count))

        def multiply(c, mb):
            for e in (2 * c, 2 * c + 1):
                for first, count in quantize_pieces(e * C, C):
                    multiply_slots(mb, first, count)
            leave_bank(mb, c * CHUNK, CHUNK)

        def products(mb, first, count):
            prods = []
            for r in range(2):
                prod = ring.tile([P, count], F32, name="prod%d_%d" % (r, count))
                nc.vector.tensor_tensor(
                    prod[:],
                    y_sb[mb][:].indirect(pos_t[r][:, first // 16:(first + count) // 16]),
                    gate_t[(r, mb)][:, first:first + count],
                    MULT,
                )
                prods.append(prod)
            return prods

        def add_on_vector(mb, prods, skip, first, count):
            res = ring.tile([P, count], F32, name="res%d" % count)
            nc.vector.tensor_tensor(res[:], prods[0][:, skip:skip + count], prods[1][:, skip:skip + count], ADD)
            nc.sync.dma_start(out[mb * P:(mb + 1) * P, first:first + count], res[:])

        def add_on_tensor(mb, prods, count):
            res = keep.tile([P, count], F32, name="res_t")
            for c in range(-(-count // CHUNK)):
                width = min(CHUNK, count - c * CHUNK)
                cols = slice(c * CHUNK, c * CHUNK + width)
                acc = psum.tile([P, CHUNK], F32, name="bank%d_%d" % (mb, c))
                for r in range(2):
                    nc.tensor.matmul(acc[:, 0:width], lhsT=ident[:], rhs=prods[r][:, cols], start=(r == 0), stop=(r == 1))
                nc.scalar.copy(res[:, cols], acc[:, 0:width])
            nc.sync.dma_start(out[mb * P:(mb + 1) * P, 0:count], res[:])

        def combine(mb, first, count):
            add_on_vector(mb, products(mb, first, count), 0, first, count)

        ident = keep.tile([P, P], F32, name="ident")
        make_identity(nc, ident[:])

        warm = keep.tile([P, 2], F32, name="warm")
        nc.vector.memset(warm[:, 0:1], 0.0)
        nc.scalar.activation(warm[:, 1:2], warm[:, 0:1], COPY)

        for t in range(PACK):
            cast(t)
        for e in range(G_EXPERTS):
            w_interleave(nc.gpsimd.tensor_copy, e)
        nc.gpsimd.tensor_copy(w_grouped[:, 1, G_EXPERTS, :, :], w_raw[G_EXPERTS][:, :, P:2 * P].rearrange("p j n -> p n j"))
        gather()
        for first, count in V_PIECES:
            merge_pairs(first, count)
        for first, count in S_PIECES:
            scalar_gather(first, count)
        for first, count in S_PIECES:
            merge_pairs(first, count)
        w_interleave_half(nc.vector.tensor_copy, G_EXPERTS, 0)
        for e in range(G_EXPERTS + 1, G_EXPERTS + 1 + S_HALVES):
            w_interleave_half(nc.vector.tensor_copy, e, 0)
            w_interleave_half(nc.scalar.copy, e, 1)
        for e in range(G_EXPERTS + 1 + S_HALVES, E):
            w_interleave_by_fours(nc.vector.tensor_copy, e)
        for h in range(2):
            w_quantize(0, h)
        for c in range(CHUNKS - 1):
            for first, count in V_PIECES + S_PIECES:
                if first // CHUNK == c:
                    x_quantize(first, count)
            multiply(c, 0)
        for e in (E - 2, E - 1):
            for first, count in quantize_pieces(e * C, C):
                x_quantize(first, count)
                multiply_slots(0, first, count)
            leave_bank(0, e * C, C)
        for h in range(2):
            w_quantize(1, h)
        for c in range(CHUNKS):
            multiply(c, 1)
        first_block = products(0, 0, T)
        add_on_tensor(0, first_block, T_SUM)
        add_on_vector(0, first_block, T_SUM, T_SUM, T - T_SUM)
        combine(1, 0, 3 * T // 4)
        combine(1, 3 * T // 4, T // 4)
